import numpy as np
import ml_dtypes

BF16 = ml_dtypes.bfloat16


def bf(x):
    return np.asarray(x, np.float32).astype(BF16)


def f32(x):
    return np.asarray(x, np.float32)


def f64(x):
    return np.asarray(x).astype(np.float64)


def striped(idx):
    return np.concatenate([l.reshape(-1, 16).T for l in idx])


def rows(idx, k):
    return np.tile(np.repeat(idx, 16, axis=0), (k // (16 * 8), 1))


def look(tab, idx):
    return np.take_along_axis(f64(tab), rows(idx, len(tab)), axis=1)


K, S, V, N, M = 128, 2048, 1024, 1024, 256


def setup_inputs():
    return {"tab": f32(np.random.standard_normal((2, K, S))), "w": bf(np.random.standard_normal((K, M)) / np.sqrt(K)), "b": f32(0.5 * np.random.standard_normal((M, 1))), "offs": striped(np.stack([np.random.permutation(S)[:N] for _ in range(8)]))}


def reference(tab, w, b, offs):
    idx = np.stack([g.T.reshape(-1) for g in np.split(offs, 8)])
    x = ((look(tab[0], idx) - 0.125) * 1.5) * (np.maximum(look(tab[1], idx), 0.0))
    return np.maximum(f64(w).T @ x + f64(b), 0.0)

@@ -1,0 +1,62 @@
+import concourse.mybir as mybir
+
+F32, BF16, U16 = mybir.dt.float32, mybir.dt.bfloat16, mybir.dt.uint16
+ALU = mybir.AluOpType
+RELU = mybir.ActivationFunctionType.Relu
+
+K, S, N, M = 128, 2048, 1024, 256
+PIECE = 512
+HALF = 128
+SHIFT, SCALE = 0.125, 1.5
+
+FLOPS = 2 * K * M * N
+
+
+def tile_lookup_vg_nrmrelu_relu_kernel(tc, tab, w, b, offs, out):
+    nc = tc.nc
+    with (
+        tc.tile_pool(name="held", bufs=1) as held,
+        tc.tile_pool(name="work", bufs=2) as work,
+        tc.psum_pool(name="psum", bufs=2) as psum,
+    ):
+        offsets = held.tile([K, N // 16], U16, name="offsets")
+        values = held.tile([K, S], F32, name="values")
+        gates = held.tile([K, S], F32, name="gates")
+        nc.sync.dma_start(offsets[:], offs)
+        nc.sync.dma_start(values[:], tab[0])
+        nc.sync.dma_start(gates[:], tab[1])
+
+        weights = held.tile([K, M], BF16, name="weights")
+        nc.scalar.dma_start(weights[:], w)
+        biases = []
+        for m in range(0, M, HALF):
+            bias = held.tile([HALF, 1], F32, name=f"bias{m}")
+            nc.scalar.dma_start(bias[:], b[m : m + HALF, :])
+            biases.append(bias)
+
+        scaled = []
+        for j in range(0, N, PIECE):
+            lists = offsets[:, j // 16 : (j + PIECE) // 16]
+            value = work.tile([K, PIECE], F32, name="value")
+            nc.vector.tensor_scalar(value[:], values[:].indirect(lists), SHIFT, SCALE, ALU.subtract, ALU.mult)
+            scaled.append(value)
+
+        products = []
+        for i, j in enumerate(range(0, N, PIECE)):
+            lists = offsets[:, j // 16 : (j + PIECE) // 16]
+            gate = work.tile([K, PIECE], F32, name="gate")
+            nc.scalar.activation(gate[:], gates[:].indirect(lists), RELU)
+            x = work.tile([K, PIECE], BF16, name="x")
+            nc.vector.tensor_tensor(x[:], scaled[i][:], gate[:], ALU.mult)
+            products.append(x)
+
+        for i, j in enumerate(range(0, N, PIECE)):
+            for h, m in enumerate(range(0, M, HALF)):
+                summed = psum.tile([HALF, PIECE], F32, name=f"summed{h}")
+                nc.tensor.matmul(summed[:], weights[:, m : m + HALF], products[i][:], start=True, stop=True)
+                result = work.tile([HALF, PIECE], F32, name=f"result{h}")
+                if h == 0:
+                    nc.scalar.activation(result[:], summed[:], RELU, bias=biases[h][:])
+                else:
+                    nc.vector.tensor_scalar(result[:], summed[:], biases[h][:], 0.0, ALU.add, ALU.max)
+                nc.sync.dma_start(out[m : m + HALF, j : j + PIECE], result[:])

@@ -34,6 +34,11 @@ def tile_lookup_vg_nrmrelu_relu_kernel(tc, tab, w, b, offs, out):
             nc.scalar.dma_start(bias[:], b[m : m + HALF, :])
             biases.append(bias)
 
+        cold = held.tile([K, 1], F32, name="cold")
+        warm = held.tile([K, 1], F32, name="warm")
+        nc.vector.memset(cold[:], 0.0)
+        nc.scalar.activation(warm[:], cold[:], RELU)
+
         scaled = []
         for j in range(0, N, PIECE):
             lists = offsets[:, j // 16 : (j + PIECE) // 16]

@@ -6,6 +6,7 @@ RELU = mybir.ActivationFunctionType.Relu
 
 K, S, N, M = 128, 2048, 1024, 256
 PIECE = 512
+CHUNK = 256
 HALF = 128
 SHIFT, SCALE = 0.125, 1.5
 
@@ -16,8 +17,8 @@ def tile_lookup_vg_nrmrelu_relu_kernel(tc, tab, w, b, offs, out):
     nc = tc.nc
     with (
         tc.tile_pool(name="held", bufs=1) as held,
-        tc.tile_pool(name="work", bufs=2) as work,
-        tc.psum_pool(name="psum", bufs=2) as psum,
+        tc.tile_pool(name="work", bufs=4) as work,
+        tc.psum_pool(name="psum", bufs=4) as psum,
     ):
         offsets = held.tile([K, N // 16], U16, name="offsets")
         values = held.tile([K, S], F32, name="values")
@@ -46,22 +47,27 @@ def tile_lookup_vg_nrmrelu_relu_kernel(tc, tab, w, b, offs, out):
             nc.vector.tensor_scalar(value[:], values[:].indirect(lists), SHIFT, SCALE, ALU.subtract, ALU.mult)
             scaled.append(value)
 
-        products = []
-        for i, j in enumerate(range(0, N, PIECE)):
+        opened = []
+        for j in range(0, N, PIECE):
             lists = offsets[:, j // 16 : (j + PIECE) // 16]
             gate = work.tile([K, PIECE], F32, name="gate")
             nc.scalar.activation(gate[:], gates[:].indirect(lists), RELU)
-            x = work.tile([K, PIECE], BF16, name="x")
-            nc.vector.tensor_tensor(x[:], scaled[i][:], gate[:], ALU.mult)
-            products.append(x)
+            opened.append(gate)
 
+        out_halves = out.rearrange("(h p) n -> p h n", p=HALF)
         for i, j in enumerate(range(0, N, PIECE)):
-            for h, m in enumerate(range(0, M, HALF)):
-                summed = psum.tile([HALF, PIECE], F32, name=f"summed{h}")
-                nc.tensor.matmul(summed[:], weights[:, m : m + HALF], products[i][:], start=True, stop=True)
-                result = work.tile([HALF, PIECE], F32, name=f"result{h}")
-                if h == 0:
-                    nc.scalar.activation(result[:], summed[:], RELU, bias=biases[h][:])
-                else:
-                    nc.vector.tensor_scalar(result[:], summed[:], biases[h][:], 0.0, ALU.add, ALU.max)
-                nc.sync.dma_start(out[m : m + HALF, j : j + PIECE], result[:])
+            products = []
+            for c in range(0, PIECE, CHUNK):
+                x = work.tile([K, CHUNK], BF16, name="x")
+                nc.vector.tensor_tensor(x[:], scaled[i][:, c : c + CHUNK], opened[i][:, c : c + CHUNK], ALU.mult)
+                products.append(x)
+            for x, c in zip(products, range(j, j + PIECE, CHUNK)):
+                result = work.tile([HALF, M // HALF, CHUNK], F32, name="result")
+                for h in range(M // HALF):
+                    summed = psum.tile([HALF, CHUNK], F32, name=f"summed{h}")
+                    nc.tensor.matmul(summed[:], weights[:, h * HALF : (h + 1) * HALF], x[:], start=True, stop=True)
+                    if h == 0:
+                        nc.scalar.activation(result[:, h, :], summed[:], RELU, bias=biases[h][:])
+                    else:
+                        nc.vector.tensor_scalar(result[:, h, :], summed[:], biases[h][:], 0.0, ALU.add, ALU.max)
+                    nc.sync.dma_start(out_halves[:, h, c : c + CHUNK], result[:, h, :])

@@ -28,11 +28,11 @@ def tile_lookup_vg_nrmrelu_relu_kernel(tc, tab, w, b, offs, out):
         nc.sync.dma_start(gates[:], tab[1])
 
         weights = held.tile([K, M], BF16, name="weights")
-        nc.scalar.dma_start(weights[:], w)
+        nc.sync.dma_start(weights[:], w)
         biases = []
         for m in range(0, M, HALF):
             bias = held.tile([HALF, 1], F32, name=f"bias{m}")
-            nc.scalar.dma_start(bias[:], b[m : m + HALF, :])
+            nc.sync.dma_start(bias[:], b[m : m + HALF, :])
             biases.append(bias)
 
         cold = held.tile([K, 1], F32, name="cold")

@@ -61,13 +61,14 @@ def tile_lookup_vg_nrmrelu_relu_kernel(tc, tab, w, b, offs, out):
                 x = work.tile([K, CHUNK], BF16, name="x")
                 nc.vector.tensor_tensor(x[:], scaled[i][:, c : c + CHUNK], opened[i][:, c : c + CHUNK], ALU.mult)
                 products.append(x)
+            last = j + PIECE == N
             for x, c in zip(products, range(j, j + PIECE, CHUNK)):
                 result = work.tile([HALF, M // HALF, CHUNK], F32, name="result")
                 for h in range(M // HALF):
                     summed = psum.tile([HALF, CHUNK], F32, name=f"summed{h}")
                     nc.tensor.matmul(summed[:], weights[:, h * HALF : (h + 1) * HALF], x[:], start=True, stop=True)
-                    if h == 0:
-                        nc.scalar.activation(result[:, h, :], summed[:], RELU, bias=biases[h][:])
-                    else:
+                    if last and h == 1:
                         nc.vector.tensor_scalar(result[:, h, :], summed[:], biases[h][:], 0.0, ALU.add, ALU.max)
+                    else:
+                        nc.scalar.activation(result[:, h, :], summed[:], RELU, bias=biases[h][:])
                     nc.sync.dma_start(out_halves[:, h, c : c + CHUNK], result[:, h, :])

import concourse.mybir as mybir

F32, BF16, U16 = mybir.dt.float32, mybir.dt.bfloat16, mybir.dt.uint16
ALU = mybir.AluOpType
RELU = mybir.ActivationFunctionType.Relu

K, S, N, M = 128, 2048, 1024, 256
PIECE = 512
CHUNK = 256
HALF = 128
SHIFT, SCALE = 0.125, 1.5

FLOPS = 2 * K * M * N


def tile_lookup_vg_nrmrelu_relu_kernel(tc, tab, w, b, offs, out):
    nc = tc.nc
    with (
        tc.tile_pool(name="held", bufs=1) as held,
        tc.tile_pool(name="work", bufs=4) as work,
        tc.psum_pool(name="psum", bufs=4) as psum,
    ):
        offsets = held.tile([K, N // 16], U16, name="offsets")
        values = held.tile([K, S], F32, name="values")
        gates = held.tile([K, S], F32, name="gates")
        nc.sync.dma_start(offsets[:], offs)
        nc.sync.dma_start(values[:], tab[0])
        nc.sync.dma_start(gates[:], tab[1])

        weights = held.tile([K, M], BF16, name="weights")
        nc.sync.dma_start(weights[:], w)
        biases = []
        for m in range(0, M, HALF):
            bias = held.tile([HALF, 1], F32, name=f"bias{m}")
            nc.sync.dma_start(bias[:], b[m : m + HALF, :])
            biases.append(bias)

        cold = held.tile([K, 1], F32, name="cold")
        warm = held.tile([K, 1], F32, name="warm")
        nc.vector.memset(cold[:], 0.0)
        nc.scalar.activation(warm[:], cold[:], RELU)

        scaled = []
        for j in range(0, N, PIECE):
            lists = offsets[:, j // 16 : (j + PIECE) // 16]
            value = work.tile([K, PIECE], F32, name="value")
            nc.vector.tensor_scalar(value[:], values[:].indirect(lists), SHIFT, SCALE, ALU.subtract, ALU.mult)
            scaled.append(value)

        opened = []
        for j in range(0, N, PIECE):
            lists = offsets[:, j // 16 : (j + PIECE) // 16]
            gate = work.tile([K, PIECE], F32, name="gate")
            nc.scalar.activation(gate[:], gates[:].indirect(lists), RELU)
            opened.append(gate)

        out_halves = out.rearrange("(h p) n -> p h n", p=HALF)
        for i, j in enumerate(range(0, N, PIECE)):
            products = []
            for c in range(0, PIECE, CHUNK):
                x = work.tile([K, CHUNK], BF16, name="x")
                nc.vector.tensor_tensor(x[:], scaled[i][:, c : c + CHUNK], opened[i][:, c : c + CHUNK], ALU.mult)
                products.append(x)
            last = j + PIECE == N
            for x, c in zip(products, range(j, j + PIECE, CHUNK)):
                result = work.tile([HALF, M // HALF, CHUNK], F32, name="result")
                for h in range(M // HALF):
                    summed = psum.tile([HALF, CHUNK], F32, name=f"summed{h}")
                    nc.tensor.matmul(summed[:], weights[:, h * HALF : (h + 1) * HALF], x[:], start=True, stop=True)
                    if last and h == 1:
                        nc.vector.tensor_scalar(result[:, h, :], summed[:], biases[h][:], 0.0, ALU.add, ALU.max)
                    else:
                        nc.scalar.activation(result[:, h, :], summed[:], RELU, bias=biases[h][:])
                    nc.sync.dma_start(out_halves[:, h, c : c + CHUNK], result[:, h, :])
